import numpy as np, ml_dtypes
CORES = [1,5,17,21,33,37,49,53]
N = 8
BF = ml_dtypes.bfloat16
def gentries(a):
    return np.ascontiguousarray(a.reshape(8, 16, -1).transpose(0, 2, 1)).reshape(8, -1)
def gtable(e):
    e = np.asarray(e); return np.ascontiguousarray(e.reshape(8, -1, 16).transpose(0, 2, 1)).reshape(128, -1).astype(np.int32)
S, B, T, RO = 3264, 48, 512, 2
H, TH, NC = S + 2 * RO * B, T // 2, (S + 2 * RO * B) // 16
G8 = np.arange(8)
def parts(rng, noise, skew):
    lab = np.argsort(rng.random((8, H)), axis=1).reshape(8, NC, 16); cl = np.zeros((8, H), np.int64)
    for g in range(8): cl[g, lab[g].reshape(-1)] = np.arange(H) // 16
    o = rng.integers(0, 16, (N, 8, 15, H))
    if skew: o = (o * rng.integers(0, 17, o.shape)) >> 4
    nm = lab[G8[None, :, None, None], ((cl + 1) % NC)[None, :, None, :], o]
    if noise > 0: nm = np.where(rng.random(nm.shape) < noise, rng.integers(0, H, nm.shape), nm)
    c = (rng.integers(0, NC, (1, 8, 1)) + np.arange(N)[:, None, None] * T + np.arange(T)[None, None, :]) % NC
    loose = lab[G8[None, :, None], c, rng.integers(0, 16, (N, 8, T))]; st = loose.copy()
    fol = rng.random((N, 8, T)) < 0.6; k = rng.integers(0, 15, (N, 8, T)); qn = np.arange(N)[:, None]
    for t in range(1, T): st[:, :, t] = np.where(fol[:, :, t], nm[qn, G8[None, :], k[:, :, t], st[:, :, t - 1]], loose[:, :, t])
    if noise > 0: st = np.where(rng.random(st.shape) < noise, rng.integers(0, H, st.shape), st)
    d = {"nm": nm, "wt": rng.integers(1, 256, (N, 8, 15, H)), "st": st}
    top = np.array([12, 60, 140, 255])[rng.integers(0, 4, (N, 8, 1))]
    d["w15"] = 1 + (top * rng.random((N, 8, H))).astype(np.int64)
    d["em"] = rng.integers(0, 16, (N, 8, 16, H)); d["ob"] = rng.integers(0, 16, (N, 8, 16, T)); d["xb"] = rng.integers(0, 16, (N, 8, 16))
    for n in ("a", "b", "v"): d[n] = rng.integers(0, 256, (N, 8, RO * T))
    return d, lab
def pack(d):
    lk = np.concatenate([256 * d["nm"] + d["wt"], d["w15"][:, :, None, :]], axis=2)
    return {"lk": np.ascontiguousarray(lk.reshape(N, 128, H)).astype(np.int32), "em": d["em"].reshape(N, 128, H).astype(np.float32).astype(BF),
            "ob": d["ob"].reshape(N, 128, T).astype(np.float32).astype(BF), "xb": d["xb"].reshape(N, 128, 1).astype(np.float32).astype(BF),
            "pe": np.stack([gtable(p[:, 0::2]) for p in d["st"]]), "po": np.stack([gtable(p[:, 1::2]) for p in d["st"]]),
            "nua": d["a"].astype(np.int32), "nub": d["b"].astype(np.int32), "vd": d["v"].astype(np.int32)}
def shares(t, n):
    return t // n + (np.arange(n) < t % n)
def tight(rng, d, g, i0):
    o = 2 + rng.permutation(S - 2)[:128]; X, Y, z = o[:8], o[8:].reshape(8, 15), o[8:]
    i = np.arange(i0, TH); p = np.arange(max(i0 - 1, 0), TH); vs = np.array([255, 255, 255, 255, 255, 255, 128, 128])
    x = d["st"][:, g]; x[:, 2 * p + 1] = X[p % 8]
    y = np.full(16, 15); y[15] = 1
    x = d["ob"][:, g]; x[:, :, 2 * i] = y[:, None]
    x = d["nm"][:, g]; x[:, :, X] = Y.T
    x[:, :8, z] = X[(np.arange(8)[:, None] + np.arange(120)[None, :]) % 8]; x[:, 8:, z] = rng.integers(0, H, (N, 7, 120))
    d["xb"][:, g] = 0
    for h in range(0, 2 * RO, 2):
        for n in ("a", "b"):
            x = d[n][:, g]; x[:, h * TH + i] = 0
        x = d["v"][:, g]; x[:, h * TH + i] = vs[(i - 1) % 8]
    for r in range(N):
        m = [int(rng.integers(17, 27)), int(rng.integers(33, 40)), int(rng.integers(65, 67)), int(rng.integers(180, 186)), int(rng.choice(np.array([7, 13, 14, 26, 28]))), int(rng.choice(np.array([52, 56, 104, 112])))]
        c6 = 128 * int(rng.integers(130, 181)) + int(rng.integers(1, 64)); c7 = 128 * int(rng.integers(130, 180)) + 65 + int(rng.integers(0, 64))
        case = ((1, 255 * m[0] + 1, m[0]), (2, 255 * m[1] + 1, m[1]), (4, 255 * m[2] + 1, m[2]), (13, 255 * m[3] + 1, m[3]),
                (3, 255 * m[4], m[4]), (9, 255 * m[5], m[5]),
                (7, c6, c6), (7, c7, c7 - 1))
        for j in range(8):
            k, c, rest = case[j]
            e = np.concatenate([shares(c, k + 1), shares(rest, 14 - k)]); a = e // 15
            F = np.zeros((16, 15), np.int64)
            F[:15] = (a // 15 + (np.arange(15)[:, None] < a % 15))[rng.permutation(15)]; F[15] = e - 15 * a
            x = d["em"][r, g]; x[:, Y[j]] = F
def setup_inputs(rng):
    return pack(parts(rng, 0.05, False)[0])
def setup_inputs_spread(rng):
    d, lab = parts(rng, 0.05, True)
    d["wt"] = np.minimum(np.exp2(8 * rng.random((N, 8, 15, H))).astype(np.int64), 255); d["w15"] = np.minimum(np.exp2(8 * rng.random((N, 8, H))).astype(np.int64), 255)
    top = np.array([2, 4, 8, 16])
    d["em"] = (top[rng.integers(0, 4, (N, 8, 1, H))] * rng.random((N, 8, 16, H))).astype(np.int64)
    d["ob"] = (top[rng.integers(0, 4, (N, 8, 1, T))] * rng.random((N, 8, 16, T))).astype(np.int64)
    d["a"] = (256 * rng.random(d["a"].shape) ** 2).astype(np.int64); d["b"] = (256 * rng.random(d["b"].shape) ** 3).astype(np.int64)
    d["v"] = np.where(rng.random(d["v"].shape) < 0.5, (256 * rng.random(d["v"].shape) ** 3).astype(np.int64), 255 - (256 * rng.random(d["v"].shape) ** 3).astype(np.int64))
    return pack(d)
def setup_inputs_ends(rng):
    d, lab = parts(rng, 0.0, False)
    m = rng.random(d["nm"].shape) < 0.76; hi = rng.random(d["nm"].shape) < 0.5
    d["nm"] = np.where(m, np.where(hi, H - 1, 0), d["nm"]); d["wt"] = np.where(hi, 255, 1)
    d["w15"] = 1 + 254 * rng.integers(0, 2, (N, 8, H))
    for n in ("em", "ob", "xb"): d[n] = 15 * rng.integers(0, 2, d[n].shape)
    d["st"] = np.where(rng.random(d["st"].shape) < 0.72, (H - 1) * rng.integers(0, 2, d["st"].shape), d["st"])
    for n in ("a", "b"): d[n] = 255 * rng.integers(0, 2, d[n].shape)
    v = 255 * rng.integers(0, 2, d["v"].shape)
    d["v"] = np.where(rng.random(v.shape) < 0.78, v, rng.choice(np.array([1, 127, 128, 129, 254]), v.shape))
    d["v"][:, 7] = np.where(rng.random((N, RO * T)) < 0.4, 128, d["v"][:, 7])
    ring = np.array([H - 1, 1, H - 1, H - 2, H - 1, 1, H - 1, H - 1, H - 2, H - 1, 1, H - 1, H - 2, H - 1, H - 2])
    for c, full in ((H - 1, 15), (H - 2, 9), (1, 11)):
        d["nm"][:, 7, :, c] = ring; d["wt"][:, 7, :, c] = np.where(np.arange(15) < full, 255, 1); d["w15"][:, 7, c] = 255; d["em"][:, 7, :, c] = 15
    d["nm"][:, 7, :, 0] = 0; d["wt"][:, 7, :, 0] = 1; d["w15"][:, 7, 0] = 1; d["em"][:, 7, :, 0] = 0; d["xb"][:, 7] = 15
    d["st"][:, 7] = rng.choice(np.array([0, 0, 0, 0, H - 1, H - 1, H - 1, H - 1, H - 2, 1]), (N, T))
    d["st"][:, 7, T - 3] = H - 1; d["st"][:, 7, T - 2] = 0; d["st"][:, 7, T - 1] = H - 1; d["st"][:, 7, 0] = H - 1
    o = rng.random((N, 8, 1, T)); d["ob"] = np.where(o < 0.08, 0, d["ob"])
    d["ob"][:, 7] = np.where(o[:, 7] > 0.5, 15, d["ob"][:, 7]); d["ob"][:, 7, :, T - 2:] = 15
    for h in range(2 * RO):
        j = h * TH + TH - 1; d["a"][:, 7, j] = 0; d["b"][:, 7, j] = 0; d["v"][:, 7, j] = 128
    X, L, V = (int(c) for c in 2 + rng.permutation(S - 2)[:3]); few = np.array([0, 16, 17, 18, 255]); rk = np.arange(N)
    x = d["nm"][:, 6]; x[(x == L) | (x == V)] = 0
    d["nm"][:, 6, :, L] = V; d["nm"][:, 6, :, V] = 0; d["nm"][:, 6, 0, V] = X; d["wt"][:, 6, 0, V] = 254; d["em"][:, 6, 0::2, V] = 15
    d["nm"][:, 6, :, X] = X; d["wt"][:, 6, :, X] = 255; d["w15"][:, 6, X] = 254; d["em"][:, 6, 0::2, X] = 15; d["xb"][:, 6, 0] = 15
    x = d["st"][:, 6]; x[(x == L) | (x == V)] = 0
    d["st"][:, 6] = np.where(rng.random((N, T)) < 0.7, X, d["st"][:, 6])
    d["st"][:, 6, :3] = X; d["st"][:, 6, T - 2 * RO - 4:] = X; d["ob"][:, 6, 0, :2] = 15
    x = d["st"][:, 6]; x[:, [TH - 1, TH + 8]] = L; x[:, [TH, TH + 1, TH + 9, TH + 10]] = X
    x = d["ob"][:, 6]; x[:, :, [TH - 1, TH, TH + 1, TH + 8, TH + 9, TH + 10]] = 0
    for n in ("a", "b"): d[n][:, 6] = few[rng.integers(0, 5, (N, RO * T))]
    for h in range(2 * RO):
        i = h * TH; j = i + TH - 1
        d["b"][:, 6, i] = few[rng.integers(0, 3, N)]; d["v"][:, 6, i] = 0
        d["a"][:, 6, j] = 17 + (rk + h) % 2; d["b"][:, 6, j] = 17 + ((rk + h) >> 1) % 2
        j = i + TH // 2 + 4 * (h & 1); d["a"][:, 6, j] = 0; d["b"][:, 6, j] = 17
    tight(rng, d, 5, TH - 16)
    return pack(d)
def setup_inputs_corners(rng):
    d, lab = parts(rng, 0.0, False)
    few = np.array([1, 2, 127, 128, 129, 238, 239, 240, 254, 255])
    d["wt"] = few[rng.integers(0, 10, (N, 8, 15, H))]; d["w15"] = few[rng.integers(0, 9, (N, 8, H))]
    for n in ("a", "b"): d[n] = rng.choice(np.array([0, 1, 128, 254, 255]), d[n].shape)
    d["v"] = rng.choice(np.array([0, 1, 127, 128, 129, 254, 255]), d["v"].shape)
    d["xb"][:, :, 0] = np.maximum(d["xb"][:, :, 0], 1); d["ob"][:, :, 0] = np.maximum(d["ob"][:, :, 0], 1)
    for g in range(8):
        o = rng.permutation(H); low, odd, z0 = o[:24], o[24:24 + TH + 32], o[24 + TH + 32]
        d["nm"][:, g] = low[rng.integers(0, 24, (N, 15, H))]
        for r in range(N):
            p = d["st"][r, g]; p[0::2] = low[rng.integers(0, 24, TH)]; p[1::2] = rng.permutation(odd)[:TH]; p[T - 1] = z0
            c = (g + r) % 8; n = (0, 1, B - 1, B + 1, B, TH, B, 2)[c]; z = rng.permutation(TH)
            if c in (1, 4, 6): z = np.concatenate([np.array([TH - 1]), z[z != TH - 1]])
            shut = z[n:]
            l = np.concatenate([np.array([z0]), p[1:T - 1:2]])
            d["a"][r, g, :TH] = 0; d["a"][r, g, shut] = 255
            d["nm"][r, g, 0, l[shut]] = p[2 * shut]; d["wt"][r, g, 0, l[shut]] = 255
    return pack(d)
def setup_inputs_crowd(rng):
    d, lab = parts(rng, 0.03, False)
    for g in range(4):
        c = rng.permutation(lab[g, int(rng.integers(0, NC))])[:4]
        x = d["nm"][:, g]; x[:, :, c] = c[rng.integers(0, 4, (N, 15, 4))]
        x = d["w15"][:, g]; x[:, c] = 255
        if g < 2: d["st"][:, g] = c[0]
        if g == 1: d["st"][np.arange(N), 1, rng.integers(0, T, N)] = c[1]
        if g == 2: d["st"][:, g] = c[rng.integers(0, 4, (N, T))]
        if g == 3: d["st"][:, g] = np.where(np.arange(T) % 2 == 0, c[0], c[1])
        for n in ("a", "b"): d[n][:, g] = rng.integers(0, 30, (N, RO * T)) * rng.integers(0, 2, (N, RO * T))
    d["v"][:, 0] = 255; d["v"][:, 1] = 0
    d["ob"][:, 7, :, 1::2] = 0
    tight(rng, d, 7, 0)
    return pack(d)
def setup_inputs_calm(rng):
    d, lab = parts(rng, 0.0, False)
    d["w15"][:] = 255; d["xb"][:] = 0; d["xb"][:, :, 0] = 15; d["ob"][:, :, 0] = 0
    for g in range(8):
        for par in range(2):
            pos = 1 + rng.permutation(15)[:g % 4]
            x = d["ob"][:, g, 0]; x[:, 2 * pos + par] = 15
            for w in range(RO):
                j = (2 * w + par) * TH + pos
                x = d["v"][:, g]; x[:, j] = 255
                x = d["a"][:, g]; x[:, j] = 0
    return pack(d)
def check_ranges(d):
    bad = []
    for k, lo, hi in (("lk", 1, 256 * H - 1), ("em", 0, 15), ("ob", 0, 15), ("xb", 0, 15), ("pe", 0, H - 1), ("po", 0, H - 1), ("nua", 0, 255), ("nub", 0, 255), ("vd", 0, 255)):
        x = np.asarray(d[k]).astype(np.float64)
        if not (np.min(x) >= lo and np.max(x) <= hi): bad.append("range of " + k)
        elif np.any(x != np.floor(x)): bad.append(k + " is not whole")
    x = np.asarray(d["lk"]).astype(np.int64)
    if np.any((x & 255) == 0): bad.append("a weight of lk is 0")
    if np.any(x.reshape(N, 8, 16, H)[:, :, 15] > 255): bad.append("a leftover of lk has a name")
    return bad
def pick(tab, ix):
    return np.take_along_axis(tab, ix.reshape(8, 1, -1), 2).reshape((8, 16) + ix.shape[1:])
def reference(lk, em, ob, xb, pe, po, nua, nub, vd):
    P = lk.astype(np.int64).reshape(N, 8, 16, H); E = em.astype(np.float32).astype(np.int64).reshape(N, 8, 16, H)
    O = ob.astype(np.float32).astype(np.int64).reshape(N, 8, 16, T); base = xb.astype(np.float32).astype(np.int64).reshape(N, 8, 16)
    st = np.zeros((N, 8, T), np.int64)
    for b in range(N): st[b, :, 0::2] = gentries(pe[b]); st[b, :, 1::2] = gentries(po[b])
    na = nua.astype(np.int64); nb = nub.astype(np.int64); vv = vd.astype(np.int64)
    named = (np.arange(16) < 15)[None, :, None]; acc = np.zeros((N, 8, 16, T), np.float64)
    for h in range(2 * RO):
        w, par = h >> 1, h & 1; cut = slice(h * TH, (h + 1) * TH)
        for r in range(N):
            b = (r + w) % N; path = st[b]
            if par == 0: s, q, l = path[:, 0::2], path[:, 1::2], np.concatenate([st[(b - 1) % N][:, T - 1:], path[:, 1:T - 1:2]], axis=1)
            else: s, l, q = path[:, 1::2], path[:, 0::2], np.concatenate([path[:, 2::2], st[(b + 1) % N][:, :1]], axis=1)
            y = O[b][:, :, par::2]; v = vv[r][:, cut]
            A = pick(P[r], l); nm, wt = A >> 8, A & 255
            u = (na[r][:, cut] * np.sum(np.where(named & (nm == s[:, None, :]), wt, 0), axis=1)) >> 8
            D = pick(P[r], s)
            u2 = (nb[r][:, cut] * np.sum(np.where(named & ((D >> 8) == q[:, None, :]), D & 255, 0), axis=1)) >> 8
            C = pick(P[r], nm)
            hold = np.any(named[..., None] & ((C >> 8) == q[:, None, None, :]) & ((C & 255) > u2[:, None, None, :]), axis=1)
            hold[:, 15] = True
            F = pick(E[r], nm); F[:, :, 15] = base[r][:, :, None]
            e = np.sum(F * y[:, :, None, :], axis=1)
            sv = (wt > u[:, None, :]) & hold
            c = np.add.accumulate(np.where(sv, e, 0), axis=1)
            hit = 256 * c > v[:, None, :] * c[:, 15:16]; got = hit[:, 15]; k = np.argmax(hit, axis=1)
            gw = np.where(sv, 1.0, 0.5) * np.exp(e * 2.0 ** -12)
            acc[r][:, :, par::2] = 0.5 * acc[r][:, :, par::2] + np.sum(gw[:, None] * F, axis=2)
            first = np.zeros((8, TH), bool)
            for g in range(8): first[g, np.unique(l[g], return_index=True)[1]] = True
            ask = (got & (k == 15) & first).astype(np.int64); before = np.add.accumulate(ask, axis=1) - ask; born = (ask == 1) & (before < B)
            ns = np.where(got & (k < 15), np.take_along_axis(nm, k[:, None, :], 1)[:, 0], s); ns = np.where(born, S + h * B + before, ns)
            for g in range(8):
                i = np.flatnonzero(first[g] & got[g] & (k[g] < 15)); ki = k[g, i]
                P[r, g, ki, l[g, i]] = 256 * nm[g, ki, i] + np.minimum(wt[g, ki, i] + 16, 255)
                i = np.flatnonzero(born[g]); j = before[g, i]; new = S + h * B + j
                P[r, g, j & 7, l[g, i]] = 256 * new + 128
                tile = A[g][:, i]; tile[0] = 256 * q[g, i] + 128
                P[r, g][:, new] = tile; E[r, g][:, new] = y[g][:, i]
            st[b, :, par::2] = ns
    z = np.zeros((N, 8, 16, T), np.float64)
    for r in range(N):
        A = pick(P[r], st[(r + RO - 1) % N]); F = pick(E[r], A >> 8); F[:, :, 15] = base[r][:, :, None]
        z[r] = np.sum((A & 255)[:, None] * F, axis=2)
    return {"ya": acc.reshape(N, 128, T).astype(np.float32), "yz": z.reshape(N, 128, T).astype(np.float32)}

def check_inputs(d):
    bad = list(check_ranges(d))
    if not bad:
        for name, y in reference(**d).items():
            for q in range(N):
                v = np.abs(np.asarray(y[q], np.float64)); s = np.sqrt(np.mean(v * v))
                if v.max() > 8 * s or s < 2.0 ** 4: bad.append('%s of rank %d is uneven or too small' % (name, q))
    return bad

import math
from concourse.mybir import dt, AluOpType, AxisListType, ActivationFunctionType

ALU = AluOpType
ACT = ActivationFunctionType
H, S0, NB, TH = 3456, 3264, 48, 256
DUM = H + 1
M23 = 12582912.0
M31 = 3221225472.0
MB = 49408.0
CN = CL = 1728.0
CH = 4096.0 * math.log(2.0) / 2.0
CHH, CHL = 1416.0, 3.5625
EW = 272
LEAD = {"zSDX": 100, "zVOF2": 100, "aGIOT": 100, "aGLT": 50, "eVNC": 100, "eVONH": 100, "eVO3": 100, "eSNC": 100}
QUART = tuple((64 * i, 64 * i + 64) for i in range(4))
HALF = ((0, 128), (128, 256))
OPT = {"tries": 1500, "seed": 1, "dw": 1, "pz": (HALF, HALF), "pc": ((0, 128), (128, 256)), "pf": ((0, 128), (128, 256)), "eq": 2, "rl": (), "turns": 6, "late": (), "vshare": 1, "lat": 4000.0, "pe": 0.45, "g": 1.5}

F32, BF, F16, I32, U16 = "float32", "bfloat16", "float16", "int32", "uint16"
MBF = ["ONB", "N128", "IB", "I32B", "NHI", "I128", "CK", "DIF", "A15", "CHH", "CHL", "NCH", "NCL", "SGN", "BIG", "CLO", "CW"]
KU = 1408.0
MFL = ["IF", "N512", "K0", "L0", "P512", "L15", "T256", "NON", "SH", "SHA", "SHB", "B15", "HI8"]
PART = {k: ("MB", 128 * i) for i, k in enumerate(MBF)}
PART.update({k: ("MF", 128 * i) for i, k in enumerate(MFL)})
SB = {
    "LK": (H, I32), "TB": (3760, F32), "EM": (3472, BF), "IOT": (H, F32), "OB0": (512, BF), "OB1": (512, BF),
    "PIN": (32, I32), "NUI": (192, I32), "NUB": (192, BF), "ABV": (3072, F32),
    "PE0": (16, U16), "PO0": (16, U16), "PVO": (16, U16), "E0": (16, U16), "NE0": (16, U16), "O1": (16, U16),
    "NO1": (16, U16), "E2": (16, U16), "NE2": (16, U16), "O3": (16, U16),
    "CI": (16, I32), "CC": (32, F32), "X0": (304, F32), "X1": (304, F32), "X2": (304, F32), "MK": (16, F32), "ML": (16, F32),
    "MB": (128 * len(MBF), BF), "MF": (128 * len(MFL), F32), "ZB": (144, BF), "ZH": (144, F16), "IH": (640, F16),
    "X3": (256, F32), "ON4": (512, BF), "BC2": (1024, BF), "SV1": (256, BF), "BC": (2048, BF), "LT": (2048, BF), "ONE": (512, BF), "VR": (304, BF), "DROW": (256, F32), "MSK": (48, F32), "RST": (48, F32),
    "KM": (48, F32), "CM": (192, F32), "CV": (192, F32),
    "RX": (320, F32), "RS": (256, F32), "RU": (288, F16), "LF": (32, F32), "LC": (304, F32), "QQ": (256, F32), "EQ": (17 * EW, BF),
    "LSEL": (256, F16), "NF": (256, BF), "SOF": (16, U16),
    "AX": (336, F32), "DX": (256, F32), "OFF": (256, U16), "OF2": (256, U16), "CB": (512, BF), "SG": (512, BF), "ZZ": (512, F32), "U2": (256, F16),
    "NN": (256, F16), "DW": (256, F32), "T1": (256, BF), "NC": (304, F32),
    "WB": (304, F32), "WE": (304, BF), "CG": (4096, F32), "FA": (4096, BF), "FB": (4096, BF), "DB": (4096, BF), "PR": (4096, BF),
    "PH": (4096, F16), "PG": (4096, F16), "SO": (4096, F32), "SVS": (256, BF), "ES": (256, F32), "ESV": (256, F32), "E32": (256, F32),
    "HS": (256, BF), "ASK": (304, BF), "INC": (304, BF), "JK": (304, BF), "AC": (4, F32), "IDX": (4, U16), "ONH": (256, F16),
    "TT": (256, F32), "LM": (48, F32), "LS": (48, F32), "LO3": (4, U16), "GK": (48, F32),
    "R32": (512, F32), "RHI": (512, BF), "RM": (512, BF), "G15": (256, F32), "TA": (256, F32), "YA": (512, F32), "YZ": (512, F32),
    "WC": (512, BF),
}
SCRATCH = {k: ("sbuf", [128, n], d) for k, (n, d) in SB.items()}
for _b in range(8):
    SCRATCH["B%d" % _b] = ("psum", [128, 512], F32)
NLK = 7
DMAS = ["lk%d" % i for i in range(NLK)] + ["em0", "em1", "pe", "po", "ob", "na", "nb", "nv", "xb", "ya", "yz"]
ARR = ["apo", "aob", "ae0", "ao1", "ae2"]
SEMAPHORES = ["qV", "qS", "qP", "qG", "sent"] + ["d" + n for n in DMAS] + ARR


def overlap(a, b):
    if a[1] >= b[2] or b[1] >= a[2]:
        return False
    if a[3] == b[3] and a[3] > 1 and (a[1] - b[1]) % a[3] != 0:
        return False
    return True


def build(g, core, T, topo):
    rank = T.rank_of(core)
    n = len(T.cores)
    ops = []
    phase = ["a"]
    CY = 0.83
    gq = OPT["g"]

    def v(name, a=0, b=None, s=1):
        if name in PART:
            name, a = PART[name]
            b = a + 128
        if b is None:
            b = SCRATCH[name][1][1]
        ap = T[name][:, a:b] if s == 1 else T[name][:, a:b:s]
        return (ap, [(name, a, b, s)], len(range(a, b, s)), name)

    def ind(w, o):
        return (w[0].indirect(o[0]), w[1] + o[1], 16 * o[2], w[3], w[1], o[1])

    def two(x):
        return SCRATCH[x[3]][2] in (BF, F16, U16)

    def ps(x):
        return x[3][0] == "B" and len(x[3]) == 2 and x[3][1].isdigit()

    def add(eng, fn, outs, ins, cost, sem=None, lat=0.0, after=None):
        rd, wr = [], []
        for x in ins:
            if isinstance(x, tuple):
                rd += x[1]
        for x in outs:
            if len(x) > 4:
                wr += x[4]
                rd += x[5]
            else:
                wr += x[1]
        ops.append({"e": eng, "f": fn, "r": rd, "w": wr, "c": cost, "sem": sem, "lat": lat, "after": after,
                    "k": "%s%s%s" % (phase[0], eng, wr[0][0] if wr else "")})
        return len(ops) - 1

    def A(x):
        return x[0] if isinstance(x, tuple) else x

    def vcost(out, in0, per):
        if len(out) > 4:
            return 50 + CY * 3.5 * out[2]
        if len(in0) > 4:
            return 50 + CY * gq * out[2]
        return 45 + CY * max(64, per * in0[2])

    def tt(out, a, b, op):
        add("V", lambda: g.vector.tensor_tensor(out[0], a[0], b[0], op), [out], [a, b], vcost(out, a, 1 if ps(a) or ps(b) else 2))

    def ts(out, a, s1, s2, o0, o1=None):
        if o1 is None:
            f = lambda: g.vector.tensor_scalar(out[0], a[0], A(s1), None, o0)
        else:
            f = lambda: g.vector.tensor_scalar(out[0], a[0], A(s1), A(s2), o0, o1)
        add("V", f, [out], [a, s1, s2], vcost(out, a, 0.5 if two(a) and two(out) else 1))

    def cp(out, a):
        add("V", lambda: g.vector.tensor_copy(out[0], a[0]), [out], [a], vcost(out, a, 0.5 if two(a) and two(out) else 1))

    def ms(out, c):
        add("V", lambda: g.vector.memset(out[0], c), [out], [], vcost(out, out, 0.5 if two(out) else 1))

    def scan(out, d0, d1, o0, o1):
        add("V", lambda: g.vector.tensor_tensor_scan(out[0], d0[0], d1[0], 0.0, o0, o1), [out], [d0, d1],
            vcost(out, d0, 0.5 if two(d0) and two(d1) and two(out) else 1))

    def act(out, a, func=ACT.Identity, bias=0.0, scale=1.0, acc=None):
        if acc is None:
            f = lambda: g.scalar.activation(out[0], a[0], func, bias=A(bias), scale=A(scale))
        else:
            f = lambda: g.scalar.activation(out[0], a[0], func, bias=A(bias), scale=A(scale), accum_out=acc[0])
        add("S", f, [out] + ([acc] if acc else []), [a, bias, scale], 65 + CY * (gq if len(a) > 4 else 1) * out[2])

    def mm(out, l, r, st, sp):
        c = max(64, r[2]) * (4 if SCRATCH[r[3]][2] == F32 else 1)
        add("P", lambda: g.tensor.matmul(out[0], l[0], r[0], st, sp), [out], [l, r], 10 + OPT["pe"] * c)

    def grp(out, terms):
        for i, (l, r) in enumerate(terms):
            mm(out, l, r, i == 0, i == len(terms) - 1)

    def iota(out, pat, base, cm):
        if SCRATCH[out[3]][2] == I32:
            f = lambda: g.iota(out[0], pat, base, cm)
        else:
            f = lambda: g.iota(out[0], pat, base, cm, allow_small_or_imprecise_dtypes=True)
        add("G", f, [out], [], 130 + 2 * CY * out[2])

    def sel(out, a, pat, op, fill, base, cm):
        add("G", lambda: g.affine_select(out[0], a[0], pat, op, fill, base, cm), [out], [a], 170 + 2 * CY * out[2])

    def dma(q, sem, out, in_, lat):
        o = out[0] if isinstance(out, tuple) else out
        i = in_[0] if isinstance(in_, tuple) else in_
        if q == "G":
            f = lambda: g.dma_start(o, i, allow_slow_non_contiguous=True)
        elif q == "Y":
            f = lambda: g.sync.dma_start(o, i)
        else:
            f = lambda: g.scalar.dma_start(o, i)
        add(q, f, [out] if isinstance(out, tuple) else [], [in_], 1000.0 if q == "G" else 80.0, sem=("d" + sem, 16), lat=lat)

    def link(src_rank, dst_rank):
        e = topo.engines(T.cores[src_rank], T.cores[dst_rank])[:8]
        return sum(1 << x for x in e), len(e)

    def swap(sem, src, land, step, lat):
        dst = (rank + step) % n
        rid, pid = topo.addr(T.cores[dst])[:2]
        m, cnt = link(rank, dst)
        i = add("G", lambda: g.remote_dma(land[0], src[0], T.sem[sem], T.sem["sent"], pid, rid, m), [], [src], 1000.0, sem=("sent", cnt))
        add("R", None, [land], [], 0.0, sem=(sem, link((rank - step) % n, rank)[1]), lat=lat, after=i)

    col = lambda i: v("CC", i, i + 1)
    B = lambda b, a=0, e=512, s=1: v("B%d" % b, a, e, s)
    mul, sub, plus = ALU.mult, ALU.subtract, ALU.add

    dma("S", "po", v("PIN", 16, 32), T.po[:], 2000)
    dma("S", "pe", v("PIN", 0, 16), T.pe[:], 2000)
    for i in range(NLK):
        a, b = 512 * i, min(512 * i + 512, H)
        dma("Y", "lk%d" % i, v("LK", a, b), T.lk[:, a:b], 2200 + 450 * i)
    dma("S", "ob", v("OB0"), T.ob[:], 2300)
    for i, (nm, t) in enumerate((("na", T.nua), ("nb", T.nub), ("nv", T.vd))):
        dma("S", nm, v("NUI", 64 * i, 64 * i + 64), t[:], 2300)
    dma("Y", "em0", v("EM", 0, H // 2), T.em[:, 0:H // 2], 5800)
    dma("Y", "em1", v("EM", H // 2, H), T.em[:, H // 2:H], 6500)
    cp(v("PO0"), v("PIN", 16, 32))
    swap("apo", v("PO0"), v("PVO"), 1, OPT["lat"] + 2000)
    cp(v("PE0"), v("PIN", 0, 16))

    iota(v("CI", 0, 1), [[1, 1]], 0, 1)
    iota(v("X0", 0, 128), [[1, 128]], 0, -1)
    iota(v("X1", 0, 304), [[1, 304]], 0, 0)
    iota(v("IOT", 0, 432), [[1, 432]], 0, 0)
    iota(v("X2", 0, 128), [[1, 8], [0, 16]], 0, 0)
    iota(v("X2", 128, 256), [[0, 8], [1, 16]], 0, 0)
    iota(v("X2", 256, 304), [[0, 6], [1, 8]], 0, 0)
    swap("aob", v("OB0"), v("OB1"), -1, OPT["lat"] + 3000)
    dma("G", "xb", v("EM", H, H + 1), T.xb[:], 2500)
    iota(v("X3", 0, 128), [[16, 8], [0, 2], [1, 8]], 0, -1)
    iota(v("X3", 128, 256), [[16, 8], [0, 2], [1, 8]], 8, -1)
    ts(v("CI", 4, 5), v("CI", 0, 1), 15, None, ALU.bitwise_and)
    ts(v("CI", 8, 9), v("CI", 0, 1), 4, None, ALU.logical_shift_right)
    cp(col(0), v("CI", 4, 5))
    cp(col(1), v("CI", 8, 9))
    ts(v("MK"), v("X1", 0, 16), col(0), None, ALU.is_equal)
    ts(v("ML"), v("X1", 0, 16), col(0), None, ALU.is_gt)
    l0, l14, l15, k15 = v("MK", 0, 1), v("MK", 14, 15), v("MK", 15, 16), v("ML", 15, 16)
    ts(col(2), l15, 512.0 * H, -(M31 + 256.0), mul, plus)
    for i in range(1, 8):
        if i < 5:
            act(v("IOT", 432 * i, 432 * i + 432), v("IOT", 0, 432), bias=float(432 * i))
        else:
            ts(v("IOT", 432 * i, 432 * i + 432), v("IOT", 0, 432), float(432 * i), None, plus)
    ts(v("ONB"), v("X2", 0, 128), col(1), None, ALU.is_equal)
    ts(v("IF"), v("X0", 0, 128), 0.0, None, ALU.is_equal)
    ms(v("TB", H, 3760), 0.0)
    ms(v("ONE"), 1.0)
    ms(v("AX"), 0.0)
    for i in range(NLK):
        a, b = 512 * i, min(512 * i + 512, H)
        p = B(i, 0, b - a)
        ts(p, v("LK", a, b), 128.0, M31, plus, plus)
        act(p, p, bias=col(2))
        tt(v("TB", a, b), v("LK", a, b), p, plus)
    for nm, sc in (("N512", -512.0), ("L15", l15), ("CW", -512.0 * CN)):
        act(v(nm), v("IF"), scale=sc)
    for nm, sc in (("IB", 1.0), ("I32B", 32.0), ("NHI", -0.5), ("CHH", CHH), ("CHL", CHL), ("NCH", -CHH), ("NCL", -CHL)):
        act(v(nm), v("IF"), scale=sc)
    cp(v("IH", 0, 128), v("IF"))
    act(v("N128"), v("ONB"), scale=-128.0)
    act(v("NON"), v("ONB"), scale=-1.0)
    act(col(20), v("ML", 8, 9), scale=2.0, bias=-1.0)
    act(col(21), v("ML", 8, 9), scale=-1.0, bias=1.0)
    act(v("I128"), v("ONB"), scale=8.0)
    act(v("SGN"), v("IF"), scale=col(20))
    act(v("HI8"), v("IF"), scale=col(21))
    sel(v("ON4"), v("ONE"), [[0, 4], [-16, 8], [0, 16]], ALU.is_ge, 0.0, 0, 1)
    for k in range(0, 16, 4):
        lanes = [[1, 4], [16, 8], [0, 16]]
        sel(v("BC", 128 * k, 128 * k + 512), v("ONE"), lanes, ALU.is_equal, 0.0, k, -1)
        sel(v("LT", 128 * k, 128 * k + 512), v("ON4"), lanes, ALU.is_gt, 0.0, k, -1)
        if k < 8:
            sel(v("BC2", 128 * k, 128 * k + 512), v("BC", 128 * k, 128 * k + 512), lanes, ALU.not_equal, 1.0, k + 8, -1)
    act(v("BIG"), v("BC2", 0, 128), scale=0.5)
    for j, nm in enumerate(("SHA", "SHB")):
        x = v("X3", 128 * j, 128 * j + 128)
        ts(v(nm), x, 1.0, k15, ALU.is_equal, mul)
        ts(x, x, 0.0, None, ALU.is_equal)
        tt(v(nm), v(nm), x, sub)
    a0 = PART["SHA"][1]
    ts(v("MF", a0, a0 + 128, 8), v("MB", 0, 128, 8), l15, None, mul)
    act(col(3), l0, scale=-1.0, bias=1.0)
    act(col(4), l0, scale=512.0)
    act(col(5), l0, scale=128.0 + 512.0 * CN)
    act(col(7), l15, bias=-64.5)
    act(col(9), l15, scale=-CN)
    act(col(10), l15, scale=-16.0, bias=-239.0)
    if OPT["dw"]:
        act(col(23), col(10), scale=-1.0)
    else:
        act(col(19), k15, scale=-16.0)
    act(col(6), l0, scale=128.0 - MB - KU)
    act(col(8), v("MK", 1, 2), scale=0.5, bias=col(6))
    act(col(15), v("MK", 2, 3), scale=512.0 * CN, bias=col(8))
    act(v("CLO"), v("ONB"), scale=col(15))
    ts(v("IH", 128, 256), v("IF"), -512.0, None, mul)
    ts(v("IH", 256, 384), v("IF"), k15, None, mul)
    act(col(22), l15, scale=0.5)
    act(col(11), l14, scale=-0.5, bias=col(22))
    act(col(12), l0, scale=0.5, bias=col(22))
    act(col(13), k15, scale=-0.5)
    act(col(14), col(1), scale=16.0, bias=15.0)
    for c in range(3):
        act(col(16 + c), col(0), scale=-1.0, bias=-(16.0 * c + 0.5))
    act(v("K0"), v("IF"), scale=col(3))
    ts(v("IH", 384, 512), v("IF"), 512.0, None, mul)
    ts(v("IH", 512, 640), v("IF"), col(4), None, mul)
    act(v("CK"), v("IF"), scale=col(12))
    act(v("A15"), v("ONB"), scale=col(11))
    ts(v("ZB"), v("X1", 0, 144), col(14), None, ALU.is_equal)
    ts(v("ZH"), v("X1", 0, 144), col(14), None, ALU.is_equal)
    ts(v("T256"), v("X2", 128, 256), col(0), 256.0, ALU.is_ge, mul)
    tt(v("T256"), v("T256"), v("ONB"), mul)
    ts(v("X0", 128, 256), v("X0", 0, 128), 1.0, k15, ALU.is_equal, mul)
    tt(v("SH"), v("X0", 128, 256), v("IF"), sub)
    act(v("DIF"), v("SH"), scale=col(13))
    BCk = lambda k: v("BC", 128 * k, 128 * k + 128)
    act(v("VR"), v("X1"), ACT.Relu, bias=-255.0)
    act(v("DROW"), v("X1", 0, 256), bias=DUM - CL)
    act(v("LC", 256, 304), v("X1", 0, 48), bias=DUM - CL)
    ts(v("MSK"), v("X2", 128, 176), col(0), None, ALU.is_equal)
    ts(v("RST"), v("X2", 128, 176), 0.5, None, ALU.is_gt)
    ts(v("KM"), v("X2", 256, 304), col(0), None, ALU.not_equal)
    act(v("CM"), v("X1", 0, 192), bias=S0 - CN)
    act(v("CV"), v("X1", 0, 192), scale=512.0, bias=512.0 * S0 + 128.0)
    act(v("GK"), v("KM"), scale=-1.0, bias=1.0)
    for h in range(4):
        tt(v("CV", 48 * h, 48 * h + 48), v("CV", 48 * h, 48 * h + 48), v("GK"), mul)
    ms(v("ASK", 256, 304), 0.0)
    ms(v("NC", 256, 304), 0.0)
    cp(v("NUB"), v("NUI"))

    def chance(h):
        for t in range(3):
            for r in range(4):
                bk = 6 if h else 7
                mm(B(bk, 256 * (t % 2) + 64 * r, 256 * (t % 2) + 64 * r + 64), BCk(4 * h + r), v("NUB", 64 * t, 64 * t + 64), True, True)
            if t == 1:
                act(v("ABV", 768 * h, 768 * h + 512), B(bk), scale=1.0 / 256)
        act(v("ABV", 768 * h + 512, 768 * h + 768), B(bk, 0, 256))
    for b in (4, 5):
        ms(B(b, 0, 512, 16), 0.0)

    tbw, emw, iow = v("TB", 0, H + 1), v("EM", 0, H + 1), v("IOT")
    Z = lambda nm, k: v(nm, 15 - k, 143 - k)
    Aa = v("AX", 32, 288)

    def tolist(out, src, bank, c):
        o = B(bank, 256, 272)
        grp(o, [(Z("ZH", r), v(src, r, 256, 16)) for r in range(16)])
        ts(out, o, 1.0 / 16 if src == "LSEL" else 1.0, c, mul, plus)

    def weights(bank, off, a):
        ts(v("NN"), v(off), -CN, None, plus)
        grp(bank, [(v("CW"), v("ONE", 0, 256)), (v("IF"), a), (v("IH", 128, 256), v("NN"))])

    def gcopy(out, a):
        sel(out, a, [[0, out[2]]], ALU.is_ge, 0.0, 0, 0)

    def ratios(b):
        grp(B(b, 0, 256), [(v("SHA"), v("E32"))])
        grp(B(b, 256, 512), [(v("SHB"), v("E32"))])
        act(v("R32"), B(b), ACT.Exp, scale=1.0 / 4096)
        act(v("RHI"), v("R32"))
        grp(B(b), [(v("HI8"), v("R32")), (v("SGN"), v("RHI"))])
        act(v("RM"), B(b))

    def sums(h):
        F = "FA" if h % 2 == 0 else "FB"
        for c in range(8):
            b = 4 + c % 2
            for k in range(1, 16):
                j, a = k % 8, 256 * (k // 8) + 32 * c
                mm(B(b, k, 512, 16), v("BC2", 128 * j, 128 * j + 128), v("RM", a, a + 32), True, True)
            scan(v("SO", 512 * c, 512 * c + 512), B(b), v(F, 512 * c, 512 * c + 512), mul, plus)
        ya = v("YA", h % 2, 512, 2)
        g15 = B(6 if h < 3 else 4, 256, 512)
        mm(g15, v("BIG") if h < 2 else v("BC2", 0, 128), v("RM", 0, 256), True, True)
        if h < 2:
            tt(ya, v("SO", 15, 4096, 16), g15, mul)
        else:
            tt(v("TA"), v("SO", 15, 4096, 16), g15, mul)
            tt(ya, ya, v("TA"), plus)

    plan = (("PVO", "PO0", "PE0", "E0", "ae0", "NE0"), ("NE0", "E0", "PO0", "O1", "ao1", "NO1"),
            ("O1", "NO1", "NE0", "E2", "ae2", "NE2"), ("NE2", "E2", "NO1", "O3", None, None))
    for h in range(4):
        edge, main, own, new, sem, land = plan[h]
        par = h % 2
        phase[0] = "bcde"[h]
        sh = 1 - par
        F = "FA" if par == 0 else "FB"
        ob = "OB0" if h < 2 else "OB1"
        m0 = S0 + NB * h
        lrow, qrow = v("RX", 32, 288), v("RU", 1, 257)
        if h == 0:
            chance(0)
        act(v("RX", 32 + sh, 288 + sh), ind(iow, v(main)))
        if sh:
            act(v("RX", 1, 33), ind(iow, v(edge, 14, 16)))
            act(v("AX", 1, 33), ind(tbw, v(edge, 14, 16)))
        act(v("AX", 32 + sh, 288 + sh), ind(tbw, v(main)))
        ts(v("OFF"), Aa, 1.0 / 512, None, mul)
        act(v("RS"), ind(iow, v(own)))
        act(v("DX"), ind(tbw, v(own)))
        ts(v("RU", 0, 256 + sh), v("RX", 32, 288 + sh), -CN, None, plus)
        weights(B(7, 256, 512), "OFF", Aa)
        grp(B(3, 256, 512), [(v("IH", 256, 384), v("NN")), (v("L15"), v("RS"))])
        act(v("NC", 0, 256), B(3, 256, 512), bias=col(9))
        grp(B(6, 256, 512), [(v("CW"), v("ONE", 0, 256)), (v("IF"), v("DX")), (v("IH", 128, 256), qrow)])
        hi, lo = B(6, 256, 512), B(6, 0, 256)
        ts(v("CB", 256, 512), hi, 0.0, 256.0, ALU.max, ALU.min)
        ts(v("SG", 256, 512), hi, 300.0, -256.0, ALU.is_gt, mul)
        grp(hi, [(v("ONB"), v("CB", 256, 512)), (v("ONB"), v("SG", 256, 512))])
        tt(v("ZZ", 256, 512), hi, v("ABV", 768 * h + 256, 768 * h + 512), mul)
        grp(lo, [(v("N512"), v("RS")), (v("IF"), Aa)])
        ts(v("CB", 0, 256), lo, 0.0, 256.0, ALU.max, ALU.min)
        act(v("SG", 0, 256), lo, ACT.Sign, bias=-300.0)
        grp(lo, [(v("N128"), v("ONE", 0, 256)), (v("ONB"), v("CB", 0, 256)), (v("N128"), v("SG", 0, 256))])
        tt(v("ZZ", 0, 256), lo, v("ABV", 768 * h, 768 * h + 256), mul)
        ts(v("U2"), v("ZZ", 256, 512), 255.25, KU - 255.0 / 512, ALU.min, plus)
        for c in range(4):
            act(v("CG", 1024 * c, 1024 * c + 1024), ind(tbw, v("OFF", 64 * c, 64 * c + 64)))
        for c in range(4):
            act(v(F, 1024 * c, 1024 * c + 1024), ind(emw, v("OFF", 64 * c, 64 * c + 64)))
        tt(v("T1"), B(7, 256, 512), v("ZZ", 0, 256), ALU.is_gt)
        if OPT["dw"]:
            ts(v("DW"), B(7, 256, 512), col(23), 255.0, ALU.max, sub)
        else:
            act(v("DW"), B(7, 256, 512), ACT.Relu, bias=col(10))
            act(v("DW"), v("DW"), bias=col(19))
        ql = v("RU", 256, 257)
        if not sh:
            one = v("ONE", 0, 1)
            ts(v("RU", 256, 288), ind(iow, v(edge, 0, 2)), -CN, None, plus)
            grp(B(6, 0, 1), [(v("CW"), one), (v("IF"), v("DX", 255, 256)), (v("IH", 128, 256), ql)])
            ts(v("CB", 0, 1), B(6, 0, 1), 0.0, 256.0, ALU.max, ALU.min)
            ts(v("SG", 0, 1), B(6, 0, 1), 300.0, -256.0, ALU.is_gt, mul)
            grp(B(6, 0, 1), [(v("ONB"), v("CB", 0, 1)), (v("ONB"), v("SG", 0, 1))])
            ts(v("ZZ", 511, 512), B(6, 0, 1), v("ABV", 768 * h + 511, 768 * h + 512), 255.25, mul, ALU.min)
            ts(v("U2", 255, 256), v("ZZ", 511, 512), KU - 255.0 / 512, None, plus)
        grp(B(6, 256, 512), [(v("K0"), Aa), (v("IH", 512, 640), qrow)])
        act(v("WB", 0, 256), B(6, 256, 512), bias=col(5))
        gcopy(v("WE", 0, 256), v(ob, par, 512, 2))
        act(v("WE", 256, 304), v("EM", m0, m0 + NB))
        act(v("LC", 0, 256), lrow, bias=-CL)
        ts(v("LF", 0, 16), v(main), -CN, None, plus)
        terms = [(B(7, 0, 256), v("IH", 0, 128), v("RU", 0, 256))]
        if sh:
            ts(v("LF", 16, 18), v(edge, 14, 16), -CN, None, plus)
            e = v("EQ", 16 * EW, 16 * EW + 255)
            ts(e, v("RU", 1, 256), v("LF", 17, 18), 4096.0, ALU.is_equal, mul)
            terms.append((B(7, 1, 256), BCk(15), e))
        for c in range(16):
            b = 16 * c + sh
            w = 256 + sh - b
            ts(v("EQ", EW * c, EW * c + w), v("RU", b, b + w), v("LF", c, c + 1), 4096.0, ALU.is_equal, mul)
            if b + 16 < 256:
                terms.append((B(7, b + 16, 256), v("ONB"), v("EQ", EW * c + 16, EW * c + 256 - b)))
        for r in range(1, 16):
            nc = 15 if r + sh == 16 else 16
            terms.append((B(7, sh + r, sh + r + 16 * (nc - 1) + 1, 16), v("LT", 128 * r, 128 * r + 128), v("EQ", r, r + EW * (nc - 1) + 1, EW)))
        for i, (o, l, r) in enumerate(terms):
            mm(o, l, r, i == 0, i == len(terms) - 1)
        tt(v("LSEL"), B(7, 0, 256), v("DROW"), ALU.min)
        act(v("NF"), B(7, 0, 256), ACT.Sign, bias=-2000.0)
        tolist(v("SOF"), "LSEL", 7, CL)
        if h - 1 in OPT["rl"]:
            ratios(6)
        if h < 3:
            chance(h + 1)
        if h > 0:
            sums(h - 1)
        mm(B(2, 0, 256), v("I32B"), v("ONE", 0, 256), True, False)
        for s0, s1 in OPT["pc"]:
            d, q = 512 // (s1 - s0), OPT["eq"]
            m = 16 // d
            if s1 == 256:
                mm(B(2, 0, 256), v("I32B"), v("T1"), False, False)
            mm(B(1), v("CLO"), v("ONE"), True, False)
            for b in range(d):
                mm(B(1, b, 512, d), v("IH", 384, 512), v("RU", 1 + s0, 1 + s1), False, False)
            for b in range(d):
                mm(B(1, b, 512, d), v("IH", 0, 128), v("U2", s0, s1), False, b == d - 1)
            for j in range(m):
                a = 16 * s0 + 512 * j
                tt(v("DB", a, a + 512), v("CG", 16 * s0 + j, 16 * s1, m), B(1), sub)
                if j % q == q - 1:
                    d2 = v("DB", a - (q - 1) * 512, a + 512)
                    ts(d2, d2, MB, None, ALU.is_equal)
                    for jj in range(j - q + 1, j + 1):
                        a = 16 * s0 + 512 * jj
                        for b in range(d):
                            mm(B(2, s0, s1), Z("ZB", jj + m * b), v("DB", a + b, a + 512, d), False, jj == m - 1 and b == d - 1 and s1 == 256)
        act(v("SVS"), B(2, 0, 256), ACT.Sign, bias=col(7))
        act(v("SV1"), v("SVS"), bias=0.5, scale=0.5)
        mm(B(3, 0, 256), v("NCH"), v("ONE", 0, 256), True, False)
        mm(B(3, 0, 256), v("NCL"), v("ONE", 0, 256), False, False)
        for s0, s1 in OPT["pf"]:
            d = 512 // (s1 - s0)
            m = 16 // d
            for b in range(d):
                mm(B(0, b, 512, d), v("IB"), v(ob, par + 2 * s0, 2 * s1, 2), True, True)
            for j in range(m):
                a = 16 * s0 + 512 * j
                end = j == m - 1 and s1 == 256 and h not in OPT["late"]
                tt(v("PR", a, a + 512), v(F, 16 * s0 + j, 16 * s1, m), B(0), mul)
                if end:
                    mm(B(3, 0, 256), v("CHH"), v("SVS"), False, False)
                    mm(B(3, 0, 256), v("CHL"), v("SVS"), False, False)
                for b in range(d):
                    mm(B(3, s0, s1), Z("ZB", j + m * b), v("PR", a + b, a + 512, d), False, end and b == d - 1)
        if h in OPT["late"]:
            mm(B(3, 0, 256), v("CHH"), v("SVS"), False, False)
            mm(B(3, 0, 256), v("CHL"), v("SVS"), False, True)
        tt(v("ES"), B(3, 0, 256), v("SV1"), mul)
        tt(v("ESV"), v("ES"), v("ABV", 768 * h + 512, 768 * h + 768), mul)
        act(v("E32"), B(3, 0, 256))
        grp(B(2, 256, 512), [(v("T256"), v("ES")), (v("NON"), v("ESV"))])
        act(v("HS"), B(2, 256, 512), ACT.Sign, bias=-0.5)
        grp(B(0, 0, 256), [(v("NHI"), v("NF")), (v("A15"), v("HS"))])
        oh = B(3, 0, 256)
        grp(oh, [(v("CK"), v("ONE", 0, 256)), (v("DIF"), v("HS"))])
        act(v("ASK", 0, 256), B(0, 0, 256), ACT.Relu, bias=-0.5)
        tt(v("TT"), oh, v("DW"), mul)
        scan(v("INC"), v("ASK"), v("VR"), plus, ALU.max)
        for c in range(3):
            act(v("JK"), v("INC"), ACT.Sign, bias=col(16 + c), acc=v("AC", c, c + 1))
        tt(ind(v("TB"), v("SOF")), Aa, v("TT"), sub)
        idx = v("IDX", 0, 3)
        ts(idx, v("AC", 0, 3), -0.5, 152.0, mul, plus)
        cp(ind(v("NC"), idx), v("CM", 48 * h, 48 * h + 48))
        tt(v("ONH"), oh, v("NC", 0, 256), mul)
        tolist(v(new), "ONH", 7, CN)
        if sem:
            swap(sem, v(new), v(land), -1, OPT["lat"] + 2500.0 * sh)
        tt(v("LM"), ind(v("LC"), idx), v("MSK"), mul)
        tt(v("GK"), ind(v("AX", 32, 336), idx), v("KM"), mul)
        scan(v("LS"), v("RST"), v("LM"), mul, plus)
        ts(v("LO3", 0, 3), v("LS", 15, 48, 16), CL, None, plus)
        tt(ind(v("TB"), v("LO3", 0, 3)), v("GK"), v("CV", 48 * h, 48 * h + 48), plus)
        act(v("EM", m0, m0 + NB), ind(v("WE"), idx))
        act(v("WB", 256, 304), v("TB", m0, m0 + NB))
        act(v("TB", m0, m0 + NB), ind(v("WB"), idx))
        if h not in OPT["rl"]:
            ratios(1)

    phase[0] = "z"
    for par, (lst, F, off, P) in enumerate((("E2", "FA", "OFF", "PH"), ("O3", "FB", "OF2", "PG"))):
        a = v("DX") if par else Aa
        act(a, ind(tbw, v(lst)))
        ts(v(off), a, 1.0 / 512, None, mul)
        weights(B(6, 0, 256), off, a)
        act(v("WC", 256 * par, 256 * par + 256), B(6, 0, 256))
        if par == 0:
            for c in range(4):
                act(v(F, 1024 * c, 1024 * c + 1024), ind(emw, v(off, 64 * c, 64 * c + 64)), bias=-8.0)
    sums(3)
    dma("Y", "ya", T.ya[:], v("YA"), 2500)
    for c in range(4):
        o, i = v("FB", 1024 * c, 1024 * c + 1024), ind(emw, v("OF2", 64 * c, 64 * c + 64))
        if c >= 4 - OPT["vshare"]:
            ts(o, i, -8.0, None, plus)
        else:
            act(o, i, bias=-8.0)
    turn = [0]
    for par, (F, P) in enumerate((("FA", "PH"), ("FB", "PG"))):
        wc = v("WC", 256 * par, 256 * par + 256)
        acc = B(2 + par, 0, 256)
        mm(acc, v("I128"), wc, True, False)
        for s0, s1 in OPT["pz"][par]:
            w = s1 - s0
            d = 512 // w
            for j in range(16 // d):
                b = (0, 1, 7)[turn[0] % 3]
                turn[0] += 1
                a = 16 * s0 + 512 * j
                for x in range(d):
                    mm(B(b, x, 512, d), BCk(j + 16 // d * x), v("WC", 256 * par + s0, 256 * par + s1), True, True)
                tt(v(P, a, a + 512), v(F, 16 * s0 + j, 16 * s1, 16 // d), B(b), mul)
                for x in range(d):
                    mm(B(2 + par, s0, s1), v("IH", 0, 128), v(P, a + x, a + 512, d), False, s1 == 256 and j == 16 // d - 1 and x == d - 1)
        act(v("YZ", par, 512, 2), acc)
    dma("Y", "yz", T.yz[:], v("YZ"), 2500)
    return ops


def order(ops):
    hist = {}
    for i, o in enumerate(ops):
        d = set()
        if o["after"] is not None:
            d.add(o["after"])
        for acc, w in [(x, False) for x in o["r"]] + [(x, True) for x in o["w"]]:
            bank = SCRATCH[acc[0]][0] == "psum"
            lst = hist.setdefault(acc[0], [])
            for j, pa, pw in reversed(lst):
                if j == i:
                    continue
                if bank and (ops[j]["e"] != o["e"] or o["e"] == "P"):
                    d.add(j)
                    if ops[j]["e"] == o["e"]:
                        break
                elif (w or pw) and overlap(acc, pa):
                    d.add(j)
                if pw and pa[3] == 1 and pa[1] <= acc[1] and pa[2] >= acc[2] and not bank:
                    break
        for acc, w in [(x, False) for x in o["r"]] + [(x, True) for x in o["w"]]:
            lst = hist[acc[0]]
            lst.append((i, acc, w))
            if SCRATCH[acc[0]][0] == "psum" and len(lst) > 80:
                del lst[:20]
        o["d"] = d


def arrange(ops, lead, others=None):
    n = len(ops)
    succ = [[] for _ in ops]
    for i, o in enumerate(ops):
        for j in o["d"]:
            succ[j].append(i)

    def hop(j, i):
        a, b = ops[j]["e"], ops[i]["e"]
        return 0.0 if a == b == "P" or b == "R" else (60.0 if a == b else 120.0)
    pr = [0.0] * n
    for i in range(n - 1, -1, -1):
        pr[i] = ops[i]["c"] + ops[i]["lat"] + max([pr[k] + hop(i, k) for k in succ[i]] + [0.0])
    for i in range(n):
        pr[i] += 100.0 * lead.get(ops[i]["k"], 0)
    left = [len(o["d"]) for o in ops]
    rdy = [0.0] * n
    cand = {}
    for i in range(n):
        if not left[i]:
            cand.setdefault(ops[i]["e"], []).append(i)
    free = {}
    seq = []
    end = 0.0
    while len(seq) < n:
        best = None
        for e, c in cand.items():
            if c:
                t = max(free.get(e, 0.0), min(rdy[i] for i in c))
                if best is None or t < best[0]:
                    best = (t, e)
        t, e = best
        i = max((i for i in cand[e] if rdy[i] <= t + 100.0), key=lambda i: (pr[i], -i))
        cand[e].remove(i)
        t = max(t, rdy[i])
        ops[i]["t"] = t
        free[e] = t + ops[i]["c"]
        fin = free[e] + ops[i]["lat"]
        end = max(end, fin)
        seq.append(i)
        for k in succ[i]:
            rdy[k] = max(rdy[k], fin + hop(i, k))
            left[k] -= 1
            if not left[k]:
                cand.setdefault(ops[k]["e"], []).append(k)
    pred = [[(j, ops[j]["lat"] + hop(j, i)) for j in ops[i]["d"]] for i in range(n)]
    post = [[(k, ops[i]["lat"] + hop(i, k)) for k in succ[i]] for i in range(n)]
    cost = [o["c"] for o in ops]

    def place(lst, need, first):
        fin = [0.0] * n
        slots = {}
        for i in lst:
            t = first[i]
            for j, x in need[i]:
                if fin[j] + x > t:
                    t = fin[j] + x
            c = cost[i]
            if c > 0.0:
                s = slots.setdefault(ops[i]["e"], [])
                lo, hi = 0, len(s)
                while lo < hi:
                    mid = (lo + hi) // 2
                    if s[mid][1] <= t:
                        lo = mid + 1
                    else:
                        hi = mid
                while lo < len(s) and s[lo][0] < t + c - 1e-6:
                    t = max(t, s[lo][1])
                    lo += 1
                s.insert(lo, (t, t + c))
            fin[i] = t + c
        return fin
    fin = [ops[i]["t"] + cost[i] for i in range(n)]
    for _ in range(OPT["turns"]):
        back = place(sorted(range(n), key=lambda i: (-fin[i], -i)), post, [o["lat"] for o in ops])
        fin = place(sorted(range(n), key=lambda i: (-back[i], i)), pred, [0.0] * n)
        e = max(fin[i] + ops[i]["lat"] for i in range(n))
        if e < end:
            end = e
            for i in range(n):
                ops[i]["t"] = fin[i] - cost[i]
            seq = sorted(range(n), key=lambda i: (ops[i]["t"], i))
    if not others:
        return seq, end
    eng = [o["e"] for o in ops]
    sets = [([o["c"] for o in x], [[(j, x[j]["lat"] + s * hop(j, i)) for j in ops[i]["d"]] for i in range(n)]) for x, s in others]

    def worth(lst):
        total = 0.0
        for c, need in sets:
            f = [0.0] * n
            busy = {}
            for i in lst:
                t = busy.get(eng[i], 0.0)
                for j, x in need[i]:
                    if f[j] + x > t:
                        t = f[j] + x
                f[i] = busy[eng[i]] = t + c[i]
            total += max(f)
        return total
    kinds = {}
    for i, o in enumerate(ops):
        kinds.setdefault(o["k"], []).append(i)
    names = sorted(kinds)
    at = [o["t"] for o in ops]
    best = worth(seq)
    x = OPT["seed"]
    for _ in range(OPT["tries"]):
        x = (x * 1103515245 + 12345) % 2147483648
        who = kinds[names[(x >> 8) % len(names)]]
        x = (x * 1103515245 + 12345) % 2147483648
        d = (150.0, 400.0, 1000.0, 2500.0, 6000.0)[(x >> 8) % 5] * (1 if (x >> 20) % 2 else -1)
        if (x >> 14) % 3 == 0:
            who = who[len(who) // 2:] if (x >> 17) % 2 else who[:(len(who) + 1) // 2]
        key = list(at)
        for i in who:
            key[i] += d
        if d > 0:
            for i in range(who[0], n):
                for j in ops[i]["d"]:
                    if key[j] > key[i]:
                        key[i] = key[j]
        else:
            for i in range(who[-1], -1, -1):
                for j in ops[i]["d"]:
                    if key[j] > key[i]:
                        key[j] = key[i]
        fin = place(sorted(range(n), key=lambda i: (key[i], i)), pred, [0.0] * n)
        if (x >> 24) % 4 == 0:
            back = place(sorted(range(n), key=lambda i: (-fin[i], -i)), post, [o["lat"] for o in ops])
            fin = place(sorted(range(n), key=lambda i: (-back[i], i)), pred, [0.0] * n)
        t = [fin[i] - cost[i] for i in range(n)]
        lst = sorted(range(n), key=lambda i: (t[i], i))
        w = worth(lst)
        if w <= best:
            best, at, seq = w, t, lst
    for i in range(n):
        ops[i]["t"] = at[i]
    return seq, best / len(sets)


SPEEDS = (({}, 1.0), ({"g": 1.1, "pe": 0.42, "lat": 2500.0}, 0.7), ({"g": 2.0, "lat": 5000.0}, 1.3), ({"pe": 0.65, "lat": 3500.0}, 1.6))
PLAN = {}


def planned(g, core, T, topo):
    ops = build(g, core, T, topo)
    order(ops)
    if "seq" not in PLAN:
        others = []
        for o, s in SPEEDS:
            old = dict(OPT)
            OPT.update(o)
            others.append((build(g, core, T, topo), s))
            OPT.update(old)
        PLAN["seq"], PLAN["end"] = arrange(ops, LEAD, others)
        PLAN["t"] = [o["t"] for o in ops]
    for o, t in zip(ops, PLAN["t"]):
        o["t"] = t
    return ops, PLAN["seq"]


def rank_program(g, core, T, topo):
    if T.rank_of(core) is None:
        return
    ops, seq = planned(g, core, T, topo)
    q = {"V": g.vector, "S": g.scalar, "P": g.tensor, "G": g, "Y": g.sync}
    cnt = {}
    seen = {e: {} for e in q}
    for i in seq:
        o = ops[i]
        e = o["e"]
        if o["sem"] is None:
            name, inc = "q" + e, 1
        else:
            name, inc = o["sem"]
        cnt[name] = cnt.get(name, 0) + inc
        o["sig"] = (name, cnt[name])
        if e == "R":
            o["know"] = {name: cnt[name]}
            continue
        s = seen[e]
        for j in sorted(o["d"], key=lambda j: -ops[j]["t"]):
            p = ops[j]
            if p["e"] == e == "P":
                continue
            nm, val = p["sig"]
            if s.get(nm, 0) < val:
                q[e].wait_ge(T.sem[nm], val)
                for k, x in p["know"].items():
                    if s.get(k, 0) < x:
                        s[k] = x
        ins = o["f"]()
        if name != "sent":
            ins.then_inc(T.sem[name], inc)
        know = dict(s)
        know[name] = cnt[name]
        o["know"] = know
    for name, val in cnt.items():
        g.wait_ge(T.sem[name], val)
